import numpy as np
import ml_dtypes

BF16 = ml_dtypes.bfloat16


def bf(x):
    return np.asarray(x, np.float32).astype(BF16)


def f32(x):
    return np.asarray(x, np.float32)


def f64(x):
    return np.asarray(x).astype(np.float64)


def striped(idx):
    return np.tile(idx.reshape(-1, 16).T, (8, 1))


S, K, M, N, E, Q = 1024, 256, 128, 2048, 4, 512


def two_experts():
    first = np.random.permutation(S).reshape(E, S // E)
    return np.concatenate([np.random.permutation(np.concatenate([first[e], first[(e + 1) % E]])) for e in range(E)])


def setup_inputs():
    return {"table": bf(np.random.standard_normal((K, S))), "w": bf(np.random.standard_normal((E, K, M)) / np.sqrt(K)), "c": f32(0.2 + 0.8 * np.random.random_sample((1, N))), "offs": striped(two_experts())}


def reference(table, w, c, offs):
    idx = offs[:16].T.reshape(-1)
    x = f64(table)[:, idx]
    y = np.concatenate([f64(w)[e].T @ x[:, e * Q : (e + 1) * Q] for e in range(E)], axis=1)
    return y * f64(c)

@@ -1,0 +1,56 @@
+import concourse.mybir as mybir
+
+BF16, F32, U16 = mybir.dt.bfloat16, mybir.dt.float32, mybir.dt.uint16
+MULT = mybir.AluOpType.mult
+
+P = 128
+S = 1024
+K = 256
+M = 128
+N = 2048
+E = 4
+Q = N // E
+KB = K // P
+QC = Q // 16
+
+FLOPS = 2 * K * M * N
+
+
+def tile_gather_matmul_kernel(tc, table, w, c, offs, out):
+    nc = tc.nc
+    with (
+        tc.tile_pool(name="held", bufs=1) as held,
+        tc.tile_pool(name="results", bufs=E) as results,
+        tc.psum_pool(name="banks", bufs=E) as banks,
+    ):
+        offsets = held.tile([P, N // 16], U16, name="offsets")
+        nc.sync.dma_start(offsets[:], offs)
+
+        blocks = [held.tile([P, S], BF16, name="block%d" % b) for b in range(KB)]
+        nc.sync.dma_start(blocks[0][:], table[0:P, :])
+        nc.scalar.dma_start(blocks[1][:], table[P : 2 * P, :])
+
+        weights = [held.tile([P, KB, M], BF16, name="weights%d" % e) for e in range(E)]
+        for e in range(E):
+            nc.gpsimd.dma_start(weights[e][:], w[e].rearrange("(b k) m -> k b m", k=P))
+
+        gains = [held.tile([P, Q], F32, name="gains%d" % e) for e in range(E)]
+        for e in range(E):
+            queue = nc.sync if e % 2 == 0 else nc.scalar
+            queue.dma_start(gains[e][:], c[:, e * Q : (e + 1) * Q].broadcast_to([P, Q]))
+
+        for e in range(E):
+            piece = offsets[:, e * QC : (e + 1) * QC]
+            bank = banks.tile([P, Q], F32, name="bank")
+            for b in range(KB):
+                nc.tensor.matmul(
+                    bank[:],
+                    weights[e][:, b, :],
+                    blocks[b][:].indirect(piece),
+                    start=(b == 0),
+                    stop=(b == KB - 1),
+                )
+            result = results.tile([P, Q], F32, name="result")
+            nc.vector.tensor_tensor(result[:], bank[:], gains[e][:], MULT)
+            queue = nc.sync if e % 2 == 0 else nc.scalar
+            queue.dma_start(out[:, e * Q : (e + 1) * Q], result[:])

@@ -27,14 +27,15 @@ def tile_gather_matmul_kernel(tc, table, w, c, offs, out):
         nc.sync.dma_start(offsets[:], offs)
 
         blocks = [held.tile([P, S], BF16, name="block%d" % b) for b in range(KB)]
+        weights = [held.tile([P, KB, M], BF16, name="weights%d" % e) for e in range(E)]
+        gains = [held.tile([P, Q], F32, name="gains%d" % e) for e in range(E)]
+
+        nc.scalar.dma_start(weights[0][:], w[0].rearrange("(b k) m -> k b m", k=P))
         nc.sync.dma_start(blocks[0][:], table[0:P, :])
         nc.scalar.dma_start(blocks[1][:], table[P : 2 * P, :])
-
-        weights = [held.tile([P, KB, M], BF16, name="weights%d" % e) for e in range(E)]
-        for e in range(E):
-            nc.gpsimd.dma_start(weights[e][:], w[e].rearrange("(b k) m -> k b m", k=P))
-
-        gains = [held.tile([P, Q], F32, name="gains%d" % e) for e in range(E)]
+        for e in range(1, E):
+            queue = nc.sync if e % 2 == 0 else nc.scalar
+            queue.dma_start(weights[e][:], w[e].rearrange("(b k) m -> k b m", k=P))
         for e in range(E):
             queue = nc.sync if e % 2 == 0 else nc.scalar
             queue.dma_start(gains[e][:], c[:, e * Q : (e + 1) * Q].broadcast_to([P, Q]))

@@ -13,6 +13,8 @@ Q = N // E
 KB = K // P
 QC = Q // 16
 
+WARM = 4
+
 FLOPS = 2 * K * M * N
 
 
@@ -22,7 +24,14 @@ def tile_gather_matmul_kernel(tc, table, w, c, offs, out):
         tc.tile_pool(name="held", bufs=1) as held,
         tc.tile_pool(name="results", bufs=E) as results,
         tc.psum_pool(name="banks", bufs=E) as banks,
+        tc.psum_pool(name="spare", bufs=1) as spare,
     ):
+        zeros = held.tile([P, Q], BF16, name="zeros")
+        nc.vector.memset(zeros[:], 0.0)
+        unread = spare.tile([P, Q], F32, name="unread")
+        for i in range(WARM):
+            nc.tensor.matmul(unread[:], zeros[:, 0:M], zeros[:], start=True, stop=True)
+
         offsets = held.tile([P, N // 16], U16, name="offsets")
         nc.sync.dma_start(offsets[:], offs)
 

@@ -11,9 +11,8 @@ N = 2048
 E = 4
 Q = N // E
 KB = K // P
-QC = Q // 16
 
-WARM = 4
+PIECES = [(e * Q, Q) for e in range(E - 1)] + [((E - 1) * Q + h * (Q // 2), Q // 2) for h in range(2)]
 
 FLOPS = 2 * K * M * N
 
@@ -22,16 +21,9 @@ def tile_gather_matmul_kernel(tc, table, w, c, offs, out):
     nc = tc.nc
     with (
         tc.tile_pool(name="held", bufs=1) as held,
-        tc.tile_pool(name="results", bufs=E) as results,
-        tc.psum_pool(name="banks", bufs=E) as banks,
-        tc.psum_pool(name="spare", bufs=1) as spare,
+        tc.tile_pool(name="results", bufs=len(PIECES)) as results,
+        tc.psum_pool(name="banks", bufs=len(PIECES)) as banks,
     ):
-        zeros = held.tile([P, Q], BF16, name="zeros")
-        nc.vector.memset(zeros[:], 0.0)
-        unread = spare.tile([P, Q], F32, name="unread")
-        for i in range(WARM):
-            nc.tensor.matmul(unread[:], zeros[:, 0:M], zeros[:], start=True, stop=True)
-
         offsets = held.tile([P, N // 16], U16, name="offsets")
         nc.sync.dma_start(offsets[:], offs)
 
@@ -49,18 +41,20 @@ def tile_gather_matmul_kernel(tc, table, w, c, offs, out):
             queue = nc.sync if e % 2 == 0 else nc.scalar
             queue.dma_start(gains[e][:], c[:, e * Q : (e + 1) * Q].broadcast_to([P, Q]))
 
-        for e in range(E):
-            piece = offsets[:, e * QC : (e + 1) * QC]
-            bank = banks.tile([P, Q], F32, name="bank")
+        for i, (first, count) in enumerate(PIECES):
+            e = first // Q
+            bank = banks.tile([P, count], F32, name="bank")
             for b in range(KB):
                 nc.tensor.matmul(
                     bank[:],
                     weights[e][:, b, :],
-                    blocks[b][:].indirect(piece),
+                    blocks[b][:].indirect(offsets[:, first // 16 : (first + count) // 16]),
                     start=(b == 0),
                     stop=(b == KB - 1),
                 )
-            result = results.tile([P, Q], F32, name="result")
-            nc.vector.tensor_tensor(result[:], bank[:], gains[e][:], MULT)
-            queue = nc.sync if e % 2 == 0 else nc.scalar
-            queue.dma_start(out[:, e * Q : (e + 1) * Q], result[:])
+            result = results.tile([P, count], F32, name="result")
+            nc.vector.tensor_tensor(
+                result[:], bank[:], gains[e][:, first - e * Q : first - e * Q + count], MULT
+            )
+            queue = nc.sync if i % 2 == 0 else nc.scalar
+            queue.dma_start(out[:, first : first + count], result[:])

@@ -1,4 +1,5 @@
 import concourse.mybir as mybir
+from concourse.masks import make_identity
 
 BF16, F32, U16 = mybir.dt.bfloat16, mybir.dt.float32, mybir.dt.uint16
 MULT = mybir.AluOpType.mult
@@ -11,6 +12,8 @@ N = 2048
 E = 4
 Q = N // E
 KB = K // P
+CP = N // P
+TB = Q // P
 
 PIECES = [(e * Q, Q) for e in range(E - 1)] + [((E - 1) * Q + h * (Q // 2), Q // 2) for h in range(2)]
 
@@ -22,28 +25,37 @@ def tile_gather_matmul_kernel(tc, table, w, c, offs, out):
     with (
         tc.tile_pool(name="held", bufs=1) as held,
         tc.tile_pool(name="results", bufs=len(PIECES)) as results,
-        tc.psum_pool(name="banks", bufs=len(PIECES)) as banks,
+        tc.psum_pool(name="banks", bufs=CP // TB) as banks,
     ):
         offsets = held.tile([P, N // 16], U16, name="offsets")
         nc.sync.dma_start(offsets[:], offs)
 
         blocks = [held.tile([P, S], BF16, name="block%d" % b) for b in range(KB)]
         weights = [held.tile([P, KB, M], BF16, name="weights%d" % e) for e in range(E)]
-        gains = [held.tile([P, Q], F32, name="gains%d" % e) for e in range(E)]
+        c_runs = held.tile([P, CP], F32, name="c_runs")
+        identity = held.tile([P, P], F32, name="identity")
+        make_identity(nc, identity[:])
 
+        nc.scalar.dma_start(c_runs[:], c.rearrange("o (p f) -> (o p) f", f=CP))
         nc.scalar.dma_start(weights[0][:], w[0].rearrange("(b k) m -> k b m", k=P))
         nc.sync.dma_start(blocks[0][:], table[0:P, :])
         nc.scalar.dma_start(blocks[1][:], table[P : 2 * P, :])
         for e in range(1, E):
             queue = nc.sync if e % 2 == 0 else nc.scalar
             queue.dma_start(weights[e][:], w[e].rearrange("(b k) m -> k b m", k=P))
-        for e in range(E):
-            queue = nc.sync if e % 2 == 0 else nc.scalar
-            queue.dma_start(gains[e][:], c[:, e * Q : (e + 1) * Q].broadcast_to([P, Q]))
+
+        gains = held.tile([P, P, CP], F32, name="gains")
+        for t in range(CP // TB):
+            spread = banks.tile([P, TB, P], F32, name="spread", tag="bank")
+            for a in range(TB):
+                f = t * TB + a
+                nc.tensor.transpose(spread[:, a, :], c_runs[:, f : f + 1].to_broadcast([P, P]), identity[:])
+            nc.scalar.copy(gains[:, :, t * TB : (t + 1) * TB], spread[:].rearrange("m a n -> m n a"))
+        gains_flat = gains[:].rearrange("m n f -> m (n f)")
 
         for i, (first, count) in enumerate(PIECES):
             e = first // Q
-            bank = banks.tile([P, count], F32, name="bank")
+            bank = banks.tile([P, count], F32, name="bank", tag="bank")
             for b in range(KB):
                 nc.tensor.matmul(
                     bank[:],
@@ -53,8 +65,6 @@ def tile_gather_matmul_kernel(tc, table, w, c, offs, out):
                     stop=(b == KB - 1),
                 )
             result = results.tile([P, count], F32, name="result")
-            nc.vector.tensor_tensor(
-                result[:], bank[:], gains[e][:, first - e * Q : first - e * Q + count], MULT
-            )
+            nc.vector.tensor_tensor(result[:], bank[:], gains_flat[:, first : first + count], MULT)
             queue = nc.sync if i % 2 == 0 else nc.scalar
             queue.dma_start(out[:, first : first + count], result[:])

@@ -50,7 +50,7 @@ def tile_gather_matmul_kernel(tc, table, w, c, offs, out):
             for a in range(TB):
                 f = t * TB + a
                 nc.tensor.transpose(spread[:, a, :], c_runs[:, f : f + 1].to_broadcast([P, P]), identity[:])
-            nc.scalar.copy(gains[:, :, t * TB : (t + 1) * TB], spread[:].rearrange("m a n -> m n a"))
+            nc.vector.tensor_copy(gains[:, :, t * TB : (t + 1) * TB], spread[:].rearrange("m a n -> m n a"))
         gains_flat = gains[:].rearrange("m n f -> m (n f)")
 
         for i, (first, count) in enumerate(PIECES):

@@ -12,8 +12,9 @@ N = 2048
 E = 4
 Q = N // E
 KB = K // P
-CP = N // P
-TB = Q // P
+SQ = 32
+CR = N // SQ
+RE = Q // SQ
 
 PIECES = [(e * Q, Q) for e in range(E - 1)] + [((E - 1) * Q + h * (Q // 2), Q // 2) for h in range(2)]
 
@@ -25,18 +26,20 @@ def tile_gather_matmul_kernel(tc, table, w, c, offs, out):
     with (
         tc.tile_pool(name="held", bufs=1) as held,
         tc.tile_pool(name="results", bufs=len(PIECES)) as results,
-        tc.psum_pool(name="banks", bufs=CP // TB) as banks,
+        tc.psum_pool(name="banks", bufs=E) as banks,
     ):
         offsets = held.tile([P, N // 16], U16, name="offsets")
         nc.sync.dma_start(offsets[:], offs)
 
         blocks = [held.tile([P, S], BF16, name="block%d" % b) for b in range(KB)]
         weights = [held.tile([P, KB, M], BF16, name="weights%d" % e) for e in range(E)]
-        c_runs = held.tile([P, CP], F32, name="c_runs")
-        identity = held.tile([P, P], F32, name="identity")
+        c_rows = held.tile([CR, P // SQ, SQ], F32, name="c_rows")
+        identity = held.tile([CR, CR], F32, name="identity")
         make_identity(nc, identity[:])
 
-        nc.scalar.dma_start(c_runs[:], c.rearrange("o (p f) -> (o p) f", f=CP))
+        nc.scalar.dma_start(
+            c_rows[:], c.rearrange("o (r s) -> (o r) s", s=SQ).unsqueeze(1).broadcast_to([CR, P // SQ, SQ])
+        )
         nc.scalar.dma_start(weights[0][:], w[0].rearrange("(b k) m -> k b m", k=P))
         nc.sync.dma_start(blocks[0][:], table[0:P, :])
         nc.scalar.dma_start(blocks[1][:], table[P : 2 * P, :])
@@ -44,14 +47,15 @@ def tile_gather_matmul_kernel(tc, table, w, c, offs, out):
             queue = nc.sync if e % 2 == 0 else nc.scalar
             queue.dma_start(weights[e][:], w[e].rearrange("(b k) m -> k b m", k=P))
 
-        gains = held.tile([P, P, CP], F32, name="gains")
-        for t in range(CP // TB):
-            spread = banks.tile([P, TB, P], F32, name="spread", tag="bank")
-            for a in range(TB):
-                f = t * TB + a
-                nc.tensor.transpose(spread[:, a, :], c_runs[:, f : f + 1].to_broadcast([P, P]), identity[:])
-            nc.vector.tensor_copy(gains[:, :, t * TB : (t + 1) * TB], spread[:].rearrange("m a n -> m n a"))
-        gains_flat = gains[:].rearrange("m n f -> m (n f)")
+        gains = []
+        for e in range(E):
+            flipped = banks.tile([P, CR], F32, name="flipped", tag="bank")
+            nc.tensor.transpose(flipped[:], c_rows[:].rearrange("r a s -> r (a s)"), identity[:])
+            wide = held.tile([P, RE, SQ], F32, name="wide%d" % e, align_bytes=64)
+            nc.scalar.copy(wide[:], flipped[:, e * RE : (e + 1) * RE].unsqueeze(2).to_broadcast([P, RE, SQ]))
+            gain = held.tile([P, Q], F32, name="gain%d" % e, align_bytes=64)
+            nc.vector.transpose(gain[:], wide[:].rearrange("p r i -> p (r i)"))
+            gains.append(gain)
 
         for i, (first, count) in enumerate(PIECES):
             e = first // Q
@@ -65,6 +69,8 @@ def tile_gather_matmul_kernel(tc, table, w, c, offs, out):
                     stop=(b == KB - 1),
                 )
             result = results.tile([P, count], F32, name="result")
-            nc.vector.tensor_tensor(result[:], bank[:], gains_flat[:, first : first + count], MULT)
+            nc.vector.tensor_tensor(
+                result[:], bank[:], gains[e][:, first - e * Q : first - e * Q + count], MULT
+            )
             queue = nc.sync if i % 2 == 0 else nc.scalar
             queue.dma_start(out[:, first : first + count], result[:])

@@ -18,6 +18,8 @@ RE = Q // SQ
 
 PIECES = [(e * Q, Q) for e in range(E - 1)] + [((E - 1) * Q + h * (Q // 2), Q // 2) for h in range(2)]
 
+BANKS = 4
+
 FLOPS = 2 * K * M * N
 
 
@@ -26,7 +28,8 @@ def tile_gather_matmul_kernel(tc, table, w, c, offs, out):
     with (
         tc.tile_pool(name="held", bufs=1) as held,
         tc.tile_pool(name="results", bufs=len(PIECES)) as results,
-        tc.psum_pool(name="banks", bufs=E) as banks,
+        tc.psum_pool(name="banks", bufs=1) as banks,
+        tc.psum_pool(name="flips", bufs=1) as flips,
     ):
         offsets = held.tile([P, N // 16], U16, name="offsets")
         nc.sync.dma_start(offsets[:], offs)
@@ -47,10 +50,12 @@ def tile_gather_matmul_kernel(tc, table, w, c, offs, out):
             queue = nc.sync if e % 2 == 0 else nc.scalar
             queue.dma_start(weights[e][:], w[e].rearrange("(b k) m -> k b m", k=P))
 
+        flipped = flips.tile([P, CR], F32, name="flipped")
+        nc.tensor.transpose(flipped[:], c_rows[:].rearrange("r a s -> r (a s)"), identity[:])
+        fence = banks.tile([P, BANKS * Q], F32, name="fence", offset=0)
+        nc.tensor.transpose(fence[:, 0:CR], c_rows[:].rearrange("r a s -> r (a s)"), identity[:])
         gains = []
         for e in range(E):
-            flipped = banks.tile([P, CR], F32, name="flipped", tag="bank")
-            nc.tensor.transpose(flipped[:], c_rows[:].rearrange("r a s -> r (a s)"), identity[:])
             wide = held.tile([P, RE, SQ], F32, name="wide%d" % e, align_bytes=64)
             nc.scalar.copy(wide[:], flipped[:, e * RE : (e + 1) * RE].unsqueeze(2).to_broadcast([P, RE, SQ]))
             gain = held.tile([P, Q], F32, name="gain%d" % e, align_bytes=64)
@@ -59,7 +64,7 @@ def tile_gather_matmul_kernel(tc, table, w, c, offs, out):
 
         for i, (first, count) in enumerate(PIECES):
             e = first // Q
-            bank = banks.tile([P, count], F32, name="bank", tag="bank")
+            bank = banks.tile([P, count], F32, name="bank%d" % i, offset=(i % BANKS) * Q * 4)
             for b in range(KB):
                 nc.tensor.matmul(
                     bank[:],

@@ -44,11 +44,10 @@ def tile_gather_matmul_kernel(tc, table, w, c, offs, out):
             c_rows[:], c.rearrange("o (r s) -> (o r) s", s=SQ).unsqueeze(1).broadcast_to([CR, P // SQ, SQ])
         )
         nc.scalar.dma_start(weights[0][:], w[0].rearrange("(b k) m -> k b m", k=P))
-        nc.sync.dma_start(blocks[0][:], table[0:P, :])
-        nc.scalar.dma_start(blocks[1][:], table[P : 2 * P, :])
+        for b in range(KB):
+            nc.sync.dma_start(blocks[b][:], table[b * P : (b + 1) * P, :])
         for e in range(1, E):
-            queue = nc.sync if e % 2 == 0 else nc.scalar
-            queue.dma_start(weights[e][:], w[e].rearrange("(b k) m -> k b m", k=P))
+            nc.sync.dma_start(weights[e][:], w[e].rearrange("(b k) m -> k b m", k=P))
 
         flipped = flips.tile([P, CR], F32, name="flipped")
         nc.tensor.transpose(flipped[:], c_rows[:].rearrange("r a s -> r (a s)"), identity[:])

@@ -36,19 +36,19 @@ def tile_gather_matmul_kernel(tc, table, w, c, offs, out):
 
         blocks = [held.tile([P, S], BF16, name="block%d" % b) for b in range(KB)]
         weights = [held.tile([P, KB, M], BF16, name="weights%d" % e) for e in range(E)]
+        c_once = held.tile([CR, SQ], F32, name="c_once")
         c_rows = held.tile([CR, P // SQ, SQ], F32, name="c_rows")
         identity = held.tile([CR, CR], F32, name="identity")
         make_identity(nc, identity[:])
 
-        nc.scalar.dma_start(
-            c_rows[:], c.rearrange("o (r s) -> (o r) s", s=SQ).unsqueeze(1).broadcast_to([CR, P // SQ, SQ])
-        )
+        nc.scalar.dma_start(c_once[:], c.rearrange("o (r s) -> (o r) s", s=SQ))
         nc.scalar.dma_start(weights[0][:], w[0].rearrange("(b k) m -> k b m", k=P))
         for b in range(KB):
             nc.sync.dma_start(blocks[b][:], table[b * P : (b + 1) * P, :])
         for e in range(1, E):
             nc.sync.dma_start(weights[e][:], w[e].rearrange("(b k) m -> k b m", k=P))
 
+        nc.vector.tensor_copy(c_rows[:], c_once[:].unsqueeze(1).to_broadcast([CR, P // SQ, SQ]))
         flipped = flips.tile([P, CR], F32, name="flipped")
         nc.tensor.transpose(flipped[:], c_rows[:].rearrange("r a s -> r (a s)"), identity[:])
         fence = banks.tile([P, BANKS * Q], F32, name="fence", offset=0)

@@ -16,7 +16,10 @@ SQ = 32
 CR = N // SQ
 RE = Q // SQ
 
-PIECES = [(e * Q, Q) for e in range(E - 1)] + [((E - 1) * Q + h * (Q // 2), Q // 2) for h in range(2)]
+HALVED = 2
+PIECES = [(e * Q, Q) for e in range(E - HALVED)] + [
+    (e * Q + h * (Q // 2), Q // 2) for e in range(E - HALVED, E) for h in range(2)
+]
 
 BANKS = 4
 
@@ -76,5 +79,4 @@ def tile_gather_matmul_kernel(tc, table, w, c, offs, out):
             nc.vector.tensor_tensor(
                 result[:], bank[:], gains[e][:, first - e * Q : first - e * Q + count], MULT
             )
-            queue = nc.sync if i % 2 == 0 else nc.scalar
-            queue.dma_start(out[:, first : first + count], result[:])
+            nc.sync.dma_start(out[:, first : first + count], result[:])

@@ -45,11 +45,11 @@ def tile_gather_matmul_kernel(tc, table, w, c, offs, out):
         make_identity(nc, identity[:])
 
         nc.scalar.dma_start(c_once[:], c.rearrange("o (r s) -> (o r) s", s=SQ))
-        nc.scalar.dma_start(weights[0][:], w[0].rearrange("(b k) m -> k b m", k=P))
+        nc.scalar.dma_start(weights[0][:], w[0].rearrange("(k b) m -> k b m", b=KB))
         for b in range(KB):
-            nc.sync.dma_start(blocks[b][:], table[b * P : (b + 1) * P, :])
+            nc.sync.dma_start(blocks[b][:], table.rearrange("(k b) s -> b k s", b=KB)[b])
         for e in range(1, E):
-            nc.sync.dma_start(weights[e][:], w[e].rearrange("(b k) m -> k b m", k=P))
+            nc.sync.dma_start(weights[e][:], w[e].rearrange("(k b) m -> k b m", b=KB))
 
         nc.vector.tensor_copy(c_rows[:], c_once[:].unsqueeze(1).to_broadcast([CR, P // SQ, SQ]))
         flipped = flips.tile([P, CR], F32, name="flipped")

import concourse.mybir as mybir
from concourse.masks import make_identity

BF16, F32, U16 = mybir.dt.bfloat16, mybir.dt.float32, mybir.dt.uint16
MULT = mybir.AluOpType.mult

P = 128
S = 1024
K = 256
M = 128
N = 2048
E = 4
Q = N // E
KB = K // P
SQ = 32
CR = N // SQ
RE = Q // SQ

HALVED = 2
PIECES = [(e * Q, Q) for e in range(E - HALVED)] + [
    (e * Q + h * (Q // 2), Q // 2) for e in range(E - HALVED, E) for h in range(2)
]

BANKS = 4

FLOPS = 2 * K * M * N


def tile_gather_matmul_kernel(tc, table, w, c, offs, out):
    nc = tc.nc
    with (
        tc.tile_pool(name="held", bufs=1) as held,
        tc.tile_pool(name="results", bufs=len(PIECES)) as results,
        tc.psum_pool(name="banks", bufs=1) as banks,
        tc.psum_pool(name="flips", bufs=1) as flips,
    ):
        offsets = held.tile([P, N // 16], U16, name="offsets")
        nc.sync.dma_start(offsets[:], offs)

        blocks = [held.tile([P, S], BF16, name="block%d" % b) for b in range(KB)]
        weights = [held.tile([P, KB, M], BF16, name="weights%d" % e) for e in range(E)]
        c_once = held.tile([CR, SQ], F32, name="c_once")
        c_rows = held.tile([CR, P // SQ, SQ], F32, name="c_rows")
        identity = held.tile([CR, CR], F32, name="identity")
        make_identity(nc, identity[:])

        nc.scalar.dma_start(c_once[:], c.rearrange("o (r s) -> (o r) s", s=SQ))
        nc.scalar.dma_start(weights[0][:], w[0].rearrange("(k b) m -> k b m", b=KB))
        for b in range(KB):
            nc.sync.dma_start(blocks[b][:], table.rearrange("(k b) s -> b k s", b=KB)[b])
        for e in range(1, E):
            nc.sync.dma_start(weights[e][:], w[e].rearrange("(k b) m -> k b m", b=KB))

        nc.vector.tensor_copy(c_rows[:], c_once[:].unsqueeze(1).to_broadcast([CR, P // SQ, SQ]))
        flipped = flips.tile([P, CR], F32, name="flipped")
        nc.tensor.transpose(flipped[:], c_rows[:].rearrange("r a s -> r (a s)"), identity[:])
        fence = banks.tile([P, BANKS * Q], F32, name="fence", offset=0)
        nc.tensor.transpose(fence[:, 0:CR], c_rows[:].rearrange("r a s -> r (a s)"), identity[:])
        gains = []
        for e in range(E):
            wide = held.tile([P, RE, SQ], F32, name="wide%d" % e, align_bytes=64)
            nc.scalar.copy(wide[:], flipped[:, e * RE : (e + 1) * RE].unsqueeze(2).to_broadcast([P, RE, SQ]))
            gain = held.tile([P, Q], F32, name="gain%d" % e, align_bytes=64)
            nc.vector.transpose(gain[:], wide[:].rearrange("p r i -> p (r i)"))
            gains.append(gain)

        for i, (first, count) in enumerate(PIECES):
            e = first // Q
            bank = banks.tile([P, count], F32, name="bank%d" % i, offset=(i % BANKS) * Q * 4)
            for b in range(KB):
                nc.tensor.matmul(
                    bank[:],
                    weights[e][:, b, :],
                    blocks[b][:].indirect(offsets[:, first // 16 : (first + count) // 16]),
                    start=(b == 0),
                    stop=(b == KB - 1),
                )
            result = results.tile([P, count], F32, name="result")
            nc.vector.tensor_tensor(
                result[:], bank[:], gains[e][:, first - e * Q : first - e * Q + count], MULT
            )
            nc.sync.dma_start(out[:, first : first + count], result[:])
